import numpy as np
import ml_dtypes


def mxq(x, axis, fmt="e4m3"):
    dtype, down = {"e4m3": (ml_dtypes.float8_e4m3fn, 7), "e5m2": (ml_dtypes.float8_e5m2, 14)}[fmt]
    v = np.moveaxis(np.asarray(x, np.float32).astype(ml_dtypes.bfloat16).astype(np.float64), axis, -1)
    blocks = v.reshape(v.shape[:-1] + (-1, 32))
    amax = np.abs(blocks).max(-1, keepdims=True)
    byte = np.maximum(np.where(amax > 0, np.frexp(amax)[1] - 1 + 127, 0) - down, 1)
    scale = np.exp2(byte - 127.0)
    codes = (blocks / scale).astype(np.float32).astype(dtype).astype(np.float64)
    return np.moveaxis((codes * scale).reshape(v.shape), -1, axis)


WIDE = False


def mx_kscale(k):
    if not WIDE:
        return np.ones(k)
    levels = np.array([10, -10, 5, -5, 0])
    if k % 512:
        return np.exp2(np.random.permutation(np.resize(levels, k // 32))).repeat(32)
    a = np.empty((k // 512, 16))
    for p in range(k // 512):
        a[p, :8] = np.random.permutation(np.resize(levels, 8))
        for g in range(8):
            far = levels[np.abs(levels - a[p, g]) >= 10]
            a[p, g + 8] = far[np.random.randint(len(far))]
    return np.exp2(a.ravel()).repeat(32)


def f64(x):
    return np.asarray(x).astype(np.float64)


def striped(idx):
    return np.tile(idx.reshape(-1, 16).T, (8, 1)).astype(np.uint16)


def unstriped(offs):
    return offs[:16].T.reshape(-1).astype(np.int64)


def relu(v):
    return np.maximum(v, 0.0)


K, T, E, C, N = 1536, 1280, 8, 128, 128


def by_expert(wq, xq):
    return np.concatenate([wq[e].T @ xq[:, e * C:(e + 1) * C] for e in range(E)], axis=1)


def setup_inputs():
    n = np.random.standard_normal
    s = mx_kscale(K)[:, None]
    return {
        "xT": (n((K, T)) * s).astype(np.float32),
        "xr": n((N, T)).astype(np.float32),
        "w": (n((E, K, N)) / np.sqrt(K) / s[None]).astype(np.float32),
        "b": (0.3 * n((N, E))).astype(np.float32),
        "gate": np.tile(np.random.uniform(0.2, 1.0, E * C), (N, 1)).astype(np.float32),
        "offs": striped(np.random.permutation(T)[:E * C]),
    }


def reference(xT, xr, w, b, gate, offs):
    idx = unstriped(offs)
    xq = mxq(f64(xT)[:, idx], 0, "e4m3")
    y = by_expert(mxq(f64(w), 1, "e4m3"), xq)
    y = relu(y + np.repeat(f64(b), C, axis=1))
    out = f64(xr).copy()
    out[:, idx] += f64(gate) * y
    return out

@@ -1,0 +1,179 @@
+from contextlib import ExitStack
+
+import concourse.mybir as mybir
+from concourse.masks import make_identity
+
+K, T, E, C, N = 1536, 1280, 8, 128, 128
+FLOPS = 2 * K * N * E * C
+
+F32 = mybir.dt.float32
+BF16 = mybir.dt.bfloat16
+U32 = mybir.dt.uint32
+U16 = mybir.dt.uint16
+U8 = mybir.dt.uint8
+FP8X4 = mybir.dt.float8_e4m3fn_x4
+ADD = mybir.AluOpType.add
+MULT = mybir.AluOpType.mult
+RELU = mybir.ActivationFunctionType.Relu
+
+P = 128
+J = 4
+PASSES = K // (P * J)
+SLOTS = E * C
+
+LOADS = [[(0, 1280)], [(0, 768), (768, 1280)], [(0, 512), (512, 1280)]]
+CASTS = [
+    [(0, 512, "s"), (512, 1024, "v"), (1024, 1280, "v")],
+    [(0, 256, "s"), (256, 768, "s"), (768, 1024, "s"), (1024, 1280, "v")],
+    [(0, 512, "s"), (512, 1024, "s"), (1024, 1280, "v")],
+]
+W_CHUNKS = [(2 * i, 2 * i + 2) for i in range(10)] + [(20, 21), (21, 22), (22, 23), (23, 24)]
+W_ENGINE = ["v"] + ["s"] * 13
+SCATTERS = [(0, 256), (256, 512), (512, 704), (704, 864), (864, 1024)]
+
+
+def tile_moe_res_lin_relu_kernel(tc, xT, xr, w, b, gate, offs, out):
+    nc = tc.nc
+    with ExitStack() as ctx:
+        keep = ctx.enter_context(tc.tile_pool(name="keep", bufs=1))
+        ps_y = ctx.enter_context(tc.psum_pool(name="ps_y", bufs=4))
+        ps_g = ctx.enter_context(tc.psum_pool(name="ps_g", bufs=1))
+
+        offsets = keep.tile([P, SLOTS // 16], U16, name="offsets")
+        gate16 = keep.tile([P, P], F32, name="gate16")
+        bias = keep.tile([P, E], F32, name="bias")
+        nc.scalar.dma_start(out=gate16[:], in_=gate[0:16, :].rearrange("a (e c) -> (a e) c", e=E))
+        nc.scalar.dma_start(out=bias[:], in_=b)
+
+        x_view = xT.rearrange("(c p j) t -> c p j t", p=P, j=J)
+        x_raw = []
+        for c in range(PASSES):
+            for lo, hi in LOADS[c]:
+                raw = keep.tile([P, J, hi - lo], F32, name="xraw%d_%d" % (c, lo))
+                nc.sync.dma_start(out=raw[:], in_=x_view[c][:, :, lo:hi])
+                x_raw.append((c, lo, hi, raw))
+            if c == 0:
+                nc.sync.dma_start(offsets[:], offs)
+
+        ident = keep.tile([P, P], F32, name="ident")
+        make_identity(nc, ident[:])
+        x_scales = keep.tile([P, T], U8, align_bytes=64, name="x_scales")
+        nc.gpsimd.memset(x_scales[:], 0)
+        window = keep.tile([P, T], F32, name="window")
+        nc.gpsimd.memset(window[:], 0.0)
+
+        gate_cols_ps = ps_g.tile([P, P], F32, name="gate_cols_ps")
+        nc.tensor.transpose(gate_cols_ps[:], gate16[:], ident[:])
+        gate_cols = keep.tile([P, E], F32, name="gate_cols")
+        nc.scalar.copy(gate_cols[:], gate_cols_ps[:, 0:E])
+        gate_all = keep.tile([P, SLOTS], F32, name="gate_all")
+        for h in range(2):
+            gps = ps_g.tile([P, 4, P], F32, name="gps%d" % h)
+            for q in range(4):
+                e = 4 * h + q
+                nc.tensor.transpose(gps[:, q, :], gate_cols[:, e : e + 1].to_broadcast([P, P]), ident[:])
+            nc.scalar.copy(gate_all[:, 512 * h : 512 * (h + 1)], gps[:].rearrange("p q n -> p (q n)"))
+
+        def interleave(engine, dst, src):
+            o = dst.rearrange("p (g i) t -> p g t i", i=4)
+            s = src.rearrange("p t (g i) -> p g t i", i=4)
+            if engine == "v":
+                nc.vector.tensor_copy(o, s)
+            else:
+                nc.scalar.copy(o, s)
+
+        x_codes = []
+        g_codes = []
+        for c in range(PASSES):
+            x_codes.append(keep.tile([P, T], U32, align_bytes=64, name="x_codes%d" % c))
+            g_codes.append(keep.tile([P, SLOTS], U32, align_bytes=64, name="g_codes%d" % c))
+        g_scales = keep.tile([P, SLOTS], U8, align_bytes=64, name="g_scales")
+
+        def gather_codes(c, h):
+            s = slice(512 * h, 512 * (h + 1))
+            nc.vector.tensor_copy(g_codes[c][:, s], x_codes[c][:].indirect(offsets[:, 32 * h : 32 * (h + 1)]))
+
+        def gather_scales(h):
+            s = slice(512 * h, 512 * (h + 1))
+            nc.vector.tensor_copy(g_scales[:, s], x_scales[:].indirect(offsets[:, 32 * h : 32 * (h + 1)]))
+
+        for c in range(PASSES):
+            for lo, hi, engine in CASTS[c]:
+                raw = None
+                base = 0
+                for c2, rlo, rhi, r in x_raw:
+                    if c2 == c and rlo <= lo and hi <= rhi:
+                        raw = r
+                        base = rlo
+                grouped = keep.tile([P, hi - lo, J], BF16, align_bytes=64, name="xg%d_%d" % (c, lo))
+                interleave(engine, grouped[:], raw[:, :, lo - base : hi - base])
+                nc.vector.quantize_mx(
+                    out=x_codes[c][:, lo:hi].bitcast(FP8X4),
+                    scales=x_scales[4 * c : P, lo:hi],
+                    in_=grouped[:].rearrange("p w j -> p (w j)"),
+                )
+            if c < PASSES - 1:
+                gather_codes(c, 0)
+                gather_codes(c, 1)
+        gather_codes(PASSES - 1, 0)
+        gather_scales(0)
+
+        w_view = w.rearrange("e k n -> (e k) n").rearrange("(b p j) n -> p b (j n)", p=P, j=J)
+        wq = {}
+        y = keep.tile([P, SLOTS], F32, name="y")
+        xr_sb = keep.tile([P, T], F32, name="xr_sb")
+        done_experts = 0
+        done_scatters = 0
+        for (lo, hi), engine in zip(W_CHUNKS, W_ENGINE):
+            nb = hi - lo
+            if lo == 8:
+                gather_codes(PASSES - 1, 1)
+                gather_scales(1)
+            raw = keep.tile([P, nb, J, N], F32, name="w_raw%d" % lo)
+            nc.sync.dma_start(out=raw[:, 0:nb].rearrange("p b j n -> p b (j n)"), in_=w_view[:, lo:hi, :])
+            if hi == E * PASSES:
+                nc.sync.dma_start(out=xr_sb[:], in_=xr)
+            grouped = keep.tile([P, nb, N, J], BF16, align_bytes=64, name="w_grouped%d" % lo)
+            dst = grouped[:].rearrange("p b (g i) t -> p b g t i", i=4)
+            src = raw[:].rearrange("p b t (g i) -> p b g t i", i=4)
+            if engine == "v":
+                nc.vector.tensor_copy(dst, src)
+            else:
+                nc.scalar.copy(dst, src)
+            codes = keep.tile([P, nb * N], U32, align_bytes=64, name="w_codes%d" % lo)
+            scales = keep.tile([P, nb * N], U8, align_bytes=64, name="w_scales%d" % lo)
+            nc.vector.quantize_mx(
+                out=codes[:].bitcast(FP8X4),
+                scales=scales[:],
+                in_=grouped[:, 0:nb].rearrange("p b n j -> p (b n j)"),
+            )
+            for blk in range(lo, hi):
+                wq[blk] = (codes, scales, (blk - lo) * N)
+            while done_experts < E and 3 * done_experts + 3 <= hi:
+                e = done_experts
+                acc = ps_y.tile([P, C], F32, name="acc")
+                s = slice(e * C, (e + 1) * C)
+                for c in range(PASSES):
+                    codes_e, scales_e, o = wq[3 * e + c]
+                    nc.tensor.matmul_mx(
+                        out=acc[:],
+                        lhsT=codes_e[:, o : o + N].bitcast(FP8X4),
+                        lhsT_scale=scales_e[:, o : o + N],
+                        rhs=g_codes[c][:, s].bitcast(FP8X4),
+                        rhs_scale=g_scales[4 * c : P, s],
+                        start=(c == 0),
+                        stop=(c == PASSES - 1),
+                    )
+                nc.scalar.activation(y[:, s], acc[:], RELU, bias=bias[:, e : e + 1])
+                done_experts += 1
+                while done_scatters < len(SCATTERS) and SCATTERS[done_scatters][1] <= done_experts * C:
+                    a, z = SCATTERS[done_scatters]
+                    nc.vector.tensor_tensor(
+                        window[:].indirect(offsets[:, a // 16 : z // 16]), y[:, a:z], gate_all[:, a:z], MULT
+                    )
+                    done_scatters += 1
+
+        result = keep.tile([P, T], F32, name="result")
+        for lo, hi in ((0, 576), (576, 1024), (1024, 1280)):
+            nc.vector.tensor_tensor(result[:, lo:hi], window[:, lo:hi], xr_sb[:, lo:hi], ADD)
+            nc.sync.dma_start(out=out[:, lo:hi], in_=result[:, lo:hi])

@@ -17,163 +17,180 @@ MULT = mybir.AluOpType.mult
 RELU = mybir.ActivationFunctionType.Relu
 
 P = 128
-J = 4
-PASSES = K // (P * J)
+PACK = 4
+PASSES = K // (P * PACK)
 SLOTS = E * C
+BLOCKS = E * PASSES
+LIST = 16
 
-LOADS = [[(0, 1280)], [(0, 768), (768, 1280)], [(0, 512), (512, 1280)]]
-CASTS = [
-    [(0, 512, "s"), (512, 1024, "v"), (1024, 1280, "v")],
-    [(0, 256, "s"), (256, 768, "s"), (768, 1024, "s"), (1024, 1280, "v")],
-    [(0, 512, "s"), (512, 1024, "s"), (1024, 1280, "v")],
+WINDOW = T + 96
+
+SCALAR, VECTOR = "scalar", "vector"
+
+TOKEN_LOADS = [
+    [(0, 1280)],
+    [(0, 1280)],
+    [(0, 768), (768, 1280)],
 ]
-W_CHUNKS = [(2 * i, 2 * i + 2) for i in range(10)] + [(20, 21), (21, 22), (22, 23), (23, 24)]
-W_ENGINE = ["v"] + ["s"] * 13
-SCATTERS = [(0, 256), (256, 512), (512, 704), (704, 864), (864, 1024)]
+
+TOKEN_CASTS = [
+    [(0, 256, VECTOR), (256, 768, SCALAR), (768, 1280, VECTOR)],
+    [(0, 512, SCALAR), (512, 1024, VECTOR), (1024, 1280, VECTOR)],
+    [(768, 1024, VECTOR), (512, 768, SCALAR), (0, 512, SCALAR), (1024, 1280, SCALAR)],
+]
+
+WEIGHT_GROUPS = [
+    [(0, 4, SCALAR)],
+    [(4, 8, SCALAR)],
+    [(8, 12, SCALAR)],
+    [(12, 14, VECTOR)],
+    [(14, 16, SCALAR)],
+    [(16, 18, SCALAR)],
+    [(18, 20, SCALAR), (20, 22, VECTOR)],
+    [(22, 24, SCALAR)],
+]
+
+RESULT_TILES = {8: (0, 512), 22: (512, 1024)}
+
+SCATTER = 2 * C
+ADDS = [(0, 512), (512, 960), (960, 1280)]
 
 
 def tile_moe_res_lin_relu_kernel(tc, xT, xr, w, b, gate, offs, out):
     nc = tc.nc
     with ExitStack() as ctx:
         keep = ctx.enter_context(tc.tile_pool(name="keep", bufs=1))
-        ps_y = ctx.enter_context(tc.psum_pool(name="ps_y", bufs=4))
-        ps_g = ctx.enter_context(tc.psum_pool(name="ps_g", bufs=1))
+        sums = ctx.enter_context(tc.psum_pool(name="sums", bufs=4))
+        turned = ctx.enter_context(tc.psum_pool(name="turned", bufs=1))
 
-        offsets = keep.tile([P, SLOTS // 16], U16, name="offsets")
-        gate16 = keep.tile([P, P], F32, name="gate16")
+        def interleave(engine, grouped, raw):
+            if engine == VECTOR:
+                nc.vector.tensor_copy(grouped, raw)
+            else:
+                nc.scalar.copy(grouped, raw)
+
+        offsets = keep.tile([P, SLOTS // LIST], U16, name="offsets")
+        gate_rows = keep.tile([P, C], F32, name="gate_rows")
+        nc.scalar.dma_start(out=gate_rows[:], in_=gate[0 : P // E, :].rearrange("a (e c) -> (a e) c", e=E))
         bias = keep.tile([P, E], F32, name="bias")
-        nc.scalar.dma_start(out=gate16[:], in_=gate[0:16, :].rearrange("a (e c) -> (a e) c", e=E))
         nc.scalar.dma_start(out=bias[:], in_=b)
-
-        x_view = xT.rearrange("(c p j) t -> c p j t", p=P, j=J)
-        x_raw = []
+        tokens = xT.rearrange("(c p j) t -> c p j t", p=P, j=PACK)
+        token_raw = []
         for c in range(PASSES):
-            for lo, hi in LOADS[c]:
-                raw = keep.tile([P, J, hi - lo], F32, name="xraw%d_%d" % (c, lo))
-                nc.sync.dma_start(out=raw[:], in_=x_view[c][:, :, lo:hi])
-                x_raw.append((c, lo, hi, raw))
+            for lo, hi in TOKEN_LOADS[c]:
+                raw = keep.tile([P, PACK, hi - lo], F32, name="token_raw%d_%d" % (c, lo))
+                nc.sync.dma_start(out=raw[:], in_=tokens[c][:, :, lo:hi])
+                token_raw.append((c, lo, hi, raw))
             if c == 0:
                 nc.sync.dma_start(offsets[:], offs)
 
-        ident = keep.tile([P, P], F32, name="ident")
-        make_identity(nc, ident[:])
-        x_scales = keep.tile([P, T], U8, align_bytes=64, name="x_scales")
-        nc.gpsimd.memset(x_scales[:], 0)
-        window = keep.tile([P, T], F32, name="window")
-        nc.gpsimd.memset(window[:], 0.0)
+        identity = keep.tile([P, P], F32, name="identity")
+        make_identity(nc, identity[:])
+        token_scales = keep.tile([P, WINDOW], U8, align_bytes=64, name="token_scales")
+        nc.gpsimd.memset(token_scales[:], 0)
+        scattered = keep.tile([P, T], F32, name="scattered")
+        nc.gpsimd.memset(scattered[:], 0.0)
 
-        gate_cols_ps = ps_g.tile([P, P], F32, name="gate_cols_ps")
-        nc.tensor.transpose(gate_cols_ps[:], gate16[:], ident[:])
-        gate_cols = keep.tile([P, E], F32, name="gate_cols")
-        nc.scalar.copy(gate_cols[:], gate_cols_ps[:, 0:E])
+        columns = turned.tile([P, P], F32, name="columns")
+        nc.tensor.transpose(columns[:], gate_rows[:], identity[:])
+        gate_columns = keep.tile([P, E], F32, name="gate_columns")
+        nc.scalar.copy(gate_columns[:], columns[:, 0:E])
         gate_all = keep.tile([P, SLOTS], F32, name="gate_all")
-        for h in range(2):
-            gps = ps_g.tile([P, 4, P], F32, name="gps%d" % h)
-            for q in range(4):
-                e = 4 * h + q
-                nc.tensor.transpose(gps[:, q, :], gate_cols[:, e : e + 1].to_broadcast([P, P]), ident[:])
-            nc.scalar.copy(gate_all[:, 512 * h : 512 * (h + 1)], gps[:].rearrange("p q n -> p (q n)"))
+        bank = E // 2
+        for h in range(E // bank):
+            spread = turned.tile([P, bank, C], F32, name="spread%d" % h)
+            for q in range(bank):
+                e = h * bank + q
+                nc.tensor.transpose(spread[:, q, :], gate_columns[:, e : e + 1].to_broadcast([P, P]), identity[:])
+            nc.scalar.copy(gate_all[:, h * bank * C : (h + 1) * bank * C], spread[:].rearrange("p q c -> p (q c)"))
 
-        def interleave(engine, dst, src):
-            o = dst.rearrange("p (g i) t -> p g t i", i=4)
-            s = src.rearrange("p t (g i) -> p g t i", i=4)
-            if engine == "v":
-                nc.vector.tensor_copy(o, s)
-            else:
-                nc.scalar.copy(o, s)
-
-        x_codes = []
-        g_codes = []
+        token_codes = []
+        slot_codes = []
         for c in range(PASSES):
-            x_codes.append(keep.tile([P, T], U32, align_bytes=64, name="x_codes%d" % c))
-            g_codes.append(keep.tile([P, SLOTS], U32, align_bytes=64, name="g_codes%d" % c))
-        g_scales = keep.tile([P, SLOTS], U8, align_bytes=64, name="g_scales")
-
-        def gather_codes(c, h):
-            s = slice(512 * h, 512 * (h + 1))
-            nc.vector.tensor_copy(g_codes[c][:, s], x_codes[c][:].indirect(offsets[:, 32 * h : 32 * (h + 1)]))
-
-        def gather_scales(h):
-            s = slice(512 * h, 512 * (h + 1))
-            nc.vector.tensor_copy(g_scales[:, s], x_scales[:].indirect(offsets[:, 32 * h : 32 * (h + 1)]))
-
+            token_codes.append(keep.tile([P, WINDOW], U32, align_bytes=64, name="token_codes%d" % c))
+            slot_codes.append(keep.tile([P, SLOTS], U32, align_bytes=64, name="slot_codes%d" % c))
+        slot_scales = keep.tile([P, SLOTS], U8, align_bytes=64, name="slot_scales")
         for c in range(PASSES):
-            for lo, hi, engine in CASTS[c]:
-                raw = None
-                base = 0
-                for c2, rlo, rhi, r in x_raw:
-                    if c2 == c and rlo <= lo and hi <= rhi:
-                        raw = r
-                        base = rlo
-                grouped = keep.tile([P, hi - lo, J], BF16, align_bytes=64, name="xg%d_%d" % (c, lo))
-                interleave(engine, grouped[:], raw[:, :, lo - base : hi - base])
-                nc.vector.quantize_mx(
-                    out=x_codes[c][:, lo:hi].bitcast(FP8X4),
-                    scales=x_scales[4 * c : P, lo:hi],
-                    in_=grouped[:].rearrange("p w j -> p (w j)"),
+            cast = []
+            for lo, hi, engine in TOKEN_CASTS[c]:
+                [(start, raw)] = [(l, r) for p, l, h, r in token_raw if p == c and l <= lo and hi <= h]
+                grouped = keep.tile([P, hi - lo, PACK], BF16, align_bytes=64, name="token_grouped%d_%d" % (c, lo))
+                interleave(
+                    engine,
+                    grouped[:].rearrange("p (g i) j -> p g j i", i=4),
+                    raw[:, :, lo - start : hi - start].rearrange("p j (g i) -> p g j i", i=4),
                 )
-            if c < PASSES - 1:
-                gather_codes(c, 0)
-                gather_codes(c, 1)
-        gather_codes(PASSES - 1, 0)
-        gather_scales(0)
+                cast.append((lo, hi, grouped))
+            for lo, hi, grouped in cast:
+                nc.vector.quantize_mx(
+                    out=token_codes[c][:, lo:hi].bitcast(FP8X4),
+                    scales=token_scales[4 * c : P, lo:hi],
+                    in_=grouped[:].rearrange("p t j -> p (t j)"),
+                )
+            nc.vector.tensor_copy(slot_codes[c][:], token_codes[c][:].indirect(offsets[:]))
+        nc.vector.tensor_copy(slot_scales[:], token_scales[:].indirect(offsets[:]))
 
-        w_view = w.rearrange("e k n -> (e k) n").rearrange("(b p j) n -> p b (j n)", p=P, j=J)
-        wq = {}
-        y = keep.tile([P, SLOTS], F32, name="y")
-        xr_sb = keep.tile([P, T], F32, name="xr_sb")
-        done_experts = 0
-        done_scatters = 0
-        for (lo, hi), engine in zip(W_CHUNKS, W_ENGINE):
-            nb = hi - lo
-            if lo == 8:
-                gather_codes(PASSES - 1, 1)
-                gather_scales(1)
-            raw = keep.tile([P, nb, J, N], F32, name="w_raw%d" % lo)
-            nc.sync.dma_start(out=raw[:, 0:nb].rearrange("p b j n -> p b (j n)"), in_=w_view[:, lo:hi, :])
-            if hi == E * PASSES:
-                nc.sync.dma_start(out=xr_sb[:], in_=xr)
-            grouped = keep.tile([P, nb, N, J], BF16, align_bytes=64, name="w_grouped%d" % lo)
-            dst = grouped[:].rearrange("p b (g i) t -> p b g t i", i=4)
-            src = raw[:].rearrange("p b t (g i) -> p b g t i", i=4)
-            if engine == "v":
-                nc.vector.tensor_copy(dst, src)
-            else:
-                nc.scalar.copy(dst, src)
-            codes = keep.tile([P, nb * N], U32, align_bytes=64, name="w_codes%d" % lo)
-            scales = keep.tile([P, nb * N], U8, align_bytes=64, name="w_scales%d" % lo)
+        blocks = w.rearrange("e k n -> (e k) n").rearrange("(b p j) n -> p b (j n)", p=P, j=PACK)
+        weights = []
+        results = []
+        experts = 0
+        residual = keep.tile([P, T], F32, name="residual")
+        for pieces in WEIGHT_GROUPS:
+            first, end = pieces[0][0], pieces[-1][1]
+            grouped = keep.tile([P, end - first, N, PACK], BF16, align_bytes=64, name="weight_grouped%d" % first)
+            for lo, hi, engine in pieces:
+                raw = keep.tile([P, hi - lo, PACK, N], F32, name="weight_raw%d" % lo, tag="weight_raw%d" % lo)
+                nc.sync.dma_start(out=raw[:].rearrange("p b j n -> p b (j n)"), in_=blocks[:, lo:hi, :])
+                if hi == BLOCKS:
+                    nc.sync.dma_start(out=residual[:], in_=xr)
+                interleave(
+                    engine,
+                    grouped[:, lo - first : hi - first].rearrange("p b (g i) j -> p b g j i", i=4),
+                    raw[:].rearrange("p b j (g i) -> p b g j i", i=4),
+                )
+                if lo in RESULT_TILES:
+                    a, z = RESULT_TILES[lo]
+                    y = keep.tile([P, z - a], F32, name="result%d" % a, tag="weight_raw%d" % lo)
+                    results += [(y, a)] * ((z - a) // C)
+            codes = keep.tile([P, (end - first) * N], U32, align_bytes=64, name="weight_codes%d" % first)
+            scales = keep.tile([P, (end - first) * N], U8, align_bytes=64, name="weight_scales%d" % first)
             nc.vector.quantize_mx(
                 out=codes[:].bitcast(FP8X4),
                 scales=scales[:],
-                in_=grouped[:, 0:nb].rearrange("p b n j -> p (b n j)"),
+                in_=grouped[:].rearrange("p b n j -> p (b n j)"),
             )
-            for blk in range(lo, hi):
-                wq[blk] = (codes, scales, (blk - lo) * N)
-            while done_experts < E and 3 * done_experts + 3 <= hi:
-                e = done_experts
-                acc = ps_y.tile([P, C], F32, name="acc")
-                s = slice(e * C, (e + 1) * C)
+            weights += [(codes, scales, i * N) for i in range(end - first)]
+
+            for e in range(experts, min(len(weights) // PASSES, len(results))):
+                slots = slice(e * C, (e + 1) * C)
+                acc = sums.tile([N, C], F32, name="acc")
                 for c in range(PASSES):
-                    codes_e, scales_e, o = wq[3 * e + c]
+                    codes, scales, start = weights[e * PASSES + c]
                     nc.tensor.matmul_mx(
                         out=acc[:],
-                        lhsT=codes_e[:, o : o + N].bitcast(FP8X4),
-                        lhsT_scale=scales_e[:, o : o + N],
-                        rhs=g_codes[c][:, s].bitcast(FP8X4),
-                        rhs_scale=g_scales[4 * c : P, s],
+                        lhsT=codes[:, start : start + N].bitcast(FP8X4),
+                        lhsT_scale=scales[:, start : start + N],
+                        rhs=slot_codes[c][:, slots].bitcast(FP8X4),
+                        rhs_scale=slot_scales[4 * c : P, slots],
                         start=(c == 0),
                         stop=(c == PASSES - 1),
                     )
-                nc.scalar.activation(y[:, s], acc[:], RELU, bias=bias[:, e : e + 1])
-                done_experts += 1
-                while done_scatters < len(SCATTERS) and SCATTERS[done_scatters][1] <= done_experts * C:
-                    a, z = SCATTERS[done_scatters]
+                y, origin = results[e]
+                nc.scalar.activation(
+                    y[:, e * C - origin : (e + 1) * C - origin], acc[:], RELU, bias=bias[:, e : e + 1]
+                )
+                experts = e + 1
+                z = experts * C
+                if z % SCATTER == 0:
+                    a = z - SCATTER
                     nc.vector.tensor_tensor(
-                        window[:].indirect(offsets[:, a // 16 : z // 16]), y[:, a:z], gate_all[:, a:z], MULT
+                        scattered[:].indirect(offsets[:, a // LIST : z // LIST]),
+                        y[:, a - origin : z - origin],
+                        gate_all[:, a:z],
+                        MULT,
                     )
-                    done_scatters += 1
 
-        result = keep.tile([P, T], F32, name="result")
-        for lo, hi in ((0, 576), (576, 1024), (1024, 1280)):
-            nc.vector.tensor_tensor(result[:, lo:hi], window[:, lo:hi], xr_sb[:, lo:hi], ADD)
-            nc.sync.dma_start(out=out[:, lo:hi], in_=result[:, lo:hi])
+        summed = keep.tile([P, T], F32, name="summed")
+        for lo, hi in ADDS:
+            nc.vector.tensor_tensor(summed[:, lo:hi], scattered[:, lo:hi], residual[:, lo:hi], ADD)
+            nc.sync.dma_start(out=out[:, lo:hi], in_=summed[:, lo:hi])

from contextlib import ExitStack

import concourse.mybir as mybir
from concourse.masks import make_identity

K, T, E, C, N = 1536, 1280, 8, 128, 128
FLOPS = 2 * K * N * E * C

F32 = mybir.dt.float32
BF16 = mybir.dt.bfloat16
U32 = mybir.dt.uint32
U16 = mybir.dt.uint16
U8 = mybir.dt.uint8
FP8X4 = mybir.dt.float8_e4m3fn_x4
ADD = mybir.AluOpType.add
MULT = mybir.AluOpType.mult
RELU = mybir.ActivationFunctionType.Relu

P = 128
PACK = 4
PASSES = K // (P * PACK)
SLOTS = E * C
BLOCKS = E * PASSES
LIST = 16

WINDOW = T + 96

SCALAR, VECTOR = "scalar", "vector"

TOKEN_LOADS = [
    [(0, 1280)],
    [(0, 1280)],
    [(0, 768), (768, 1280)],
]

TOKEN_CASTS = [
    [(0, 256, VECTOR), (256, 768, SCALAR), (768, 1280, VECTOR)],
    [(0, 512, SCALAR), (512, 1024, VECTOR), (1024, 1280, VECTOR)],
    [(768, 1024, VECTOR), (512, 768, SCALAR), (0, 512, SCALAR), (1024, 1280, SCALAR)],
]

WEIGHT_GROUPS = [
    [(0, 4, SCALAR)],
    [(4, 8, SCALAR)],
    [(8, 12, SCALAR)],
    [(12, 14, VECTOR)],
    [(14, 16, SCALAR)],
    [(16, 18, SCALAR)],
    [(18, 20, SCALAR), (20, 22, VECTOR)],
    [(22, 24, SCALAR)],
]

RESULT_TILES = {8: (0, 512), 22: (512, 1024)}

SCATTER = 2 * C
ADDS = [(0, 512), (512, 960), (960, 1280)]


def tile_moe_res_lin_relu_kernel(tc, xT, xr, w, b, gate, offs, out):
    nc = tc.nc
    with ExitStack() as ctx:
        keep = ctx.enter_context(tc.tile_pool(name="keep", bufs=1))
        sums = ctx.enter_context(tc.psum_pool(name="sums", bufs=4))
        turned = ctx.enter_context(tc.psum_pool(name="turned", bufs=1))

        def interleave(engine, grouped, raw):
            if engine == VECTOR:
                nc.vector.tensor_copy(grouped, raw)
            else:
                nc.scalar.copy(grouped, raw)

        offsets = keep.tile([P, SLOTS // LIST], U16, name="offsets")
        gate_rows = keep.tile([P, C], F32, name="gate_rows")
        nc.scalar.dma_start(out=gate_rows[:], in_=gate[0 : P // E, :].rearrange("a (e c) -> (a e) c", e=E))
        bias = keep.tile([P, E], F32, name="bias")
        nc.scalar.dma_start(out=bias[:], in_=b)
        tokens = xT.rearrange("(c p j) t -> c p j t", p=P, j=PACK)
        token_raw = []
        for c in range(PASSES):
            for lo, hi in TOKEN_LOADS[c]:
                raw = keep.tile([P, PACK, hi - lo], F32, name="token_raw%d_%d" % (c, lo))
                nc.sync.dma_start(out=raw[:], in_=tokens[c][:, :, lo:hi])
                token_raw.append((c, lo, hi, raw))
            if c == 0:
                nc.sync.dma_start(offsets[:], offs)

        identity = keep.tile([P, P], F32, name="identity")
        make_identity(nc, identity[:])
        token_scales = keep.tile([P, WINDOW], U8, align_bytes=64, name="token_scales")
        nc.gpsimd.memset(token_scales[:], 0)
        scattered = keep.tile([P, T], F32, name="scattered")
        nc.gpsimd.memset(scattered[:], 0.0)

        columns = turned.tile([P, P], F32, name="columns")
        nc.tensor.transpose(columns[:], gate_rows[:], identity[:])
        gate_columns = keep.tile([P, E], F32, name="gate_columns")
        nc.scalar.copy(gate_columns[:], columns[:, 0:E])
        gate_all = keep.tile([P, SLOTS], F32, name="gate_all")
        bank = E // 2
        for h in range(E // bank):
            spread = turned.tile([P, bank, C], F32, name="spread%d" % h)
            for q in range(bank):
                e = h * bank + q
                nc.tensor.transpose(spread[:, q, :], gate_columns[:, e : e + 1].to_broadcast([P, P]), identity[:])
            nc.scalar.copy(gate_all[:, h * bank * C : (h + 1) * bank * C], spread[:].rearrange("p q c -> p (q c)"))

        token_codes = []
        slot_codes = []
        for c in range(PASSES):
            token_codes.append(keep.tile([P, WINDOW], U32, align_bytes=64, name="token_codes%d" % c))
            slot_codes.append(keep.tile([P, SLOTS], U32, align_bytes=64, name="slot_codes%d" % c))
        slot_scales = keep.tile([P, SLOTS], U8, align_bytes=64, name="slot_scales")
        for c in range(PASSES):
            cast = []
            for lo, hi, engine in TOKEN_CASTS[c]:
                [(start, raw)] = [(l, r) for p, l, h, r in token_raw if p == c and l <= lo and hi <= h]
                grouped = keep.tile([P, hi - lo, PACK], BF16, align_bytes=64, name="token_grouped%d_%d" % (c, lo))
                interleave(
                    engine,
                    grouped[:].rearrange("p (g i) j -> p g j i", i=4),
                    raw[:, :, lo - start : hi - start].rearrange("p j (g i) -> p g j i", i=4),
                )
                cast.append((lo, hi, grouped))
            for lo, hi, grouped in cast:
                nc.vector.quantize_mx(
                    out=token_codes[c][:, lo:hi].bitcast(FP8X4),
                    scales=token_scales[4 * c : P, lo:hi],
                    in_=grouped[:].rearrange("p t j -> p (t j)"),
                )
            nc.vector.tensor_copy(slot_codes[c][:], token_codes[c][:].indirect(offsets[:]))
        nc.vector.tensor_copy(slot_scales[:], token_scales[:].indirect(offsets[:]))

        blocks = w.rearrange("e k n -> (e k) n").rearrange("(b p j) n -> p b (j n)", p=P, j=PACK)
        weights = []
        results = []
        experts = 0
        residual = keep.tile([P, T], F32, name="residual")
        for pieces in WEIGHT_GROUPS:
            first, end = pieces[0][0], pieces[-1][1]
            grouped = keep.tile([P, end - first, N, PACK], BF16, align_bytes=64, name="weight_grouped%d" % first)
            for lo, hi, engine in pieces:
                raw = keep.tile([P, hi - lo, PACK, N], F32, name="weight_raw%d" % lo, tag="weight_raw%d" % lo)
                nc.sync.dma_start(out=raw[:].rearrange("p b j n -> p b (j n)"), in_=blocks[:, lo:hi, :])
                if hi == BLOCKS:
                    nc.sync.dma_start(out=residual[:], in_=xr)
                interleave(
                    engine,
                    grouped[:, lo - first : hi - first].rearrange("p b (g i) j -> p b g j i", i=4),
                    raw[:].rearrange("p b j (g i) -> p b g j i", i=4),
                )
                if lo in RESULT_TILES:
                    a, z = RESULT_TILES[lo]
                    y = keep.tile([P, z - a], F32, name="result%d" % a, tag="weight_raw%d" % lo)
                    results += [(y, a)] * ((z - a) // C)
            codes = keep.tile([P, (end - first) * N], U32, align_bytes=64, name="weight_codes%d" % first)
            scales = keep.tile([P, (end - first) * N], U8, align_bytes=64, name="weight_scales%d" % first)
            nc.vector.quantize_mx(
                out=codes[:].bitcast(FP8X4),
                scales=scales[:],
                in_=grouped[:].rearrange("p b n j -> p (b n j)"),
            )
            weights += [(codes, scales, i * N) for i in range(end - first)]

            for e in range(experts, min(len(weights) // PASSES, len(results))):
                slots = slice(e * C, (e + 1) * C)
                acc = sums.tile([N, C], F32, name="acc")
                for c in range(PASSES):
                    codes, scales, start = weights[e * PASSES + c]
                    nc.tensor.matmul_mx(
                        out=acc[:],
                        lhsT=codes[:, start : start + N].bitcast(FP8X4),
                        lhsT_scale=scales[:, start : start + N],
                        rhs=slot_codes[c][:, slots].bitcast(FP8X4),
                        rhs_scale=slot_scales[4 * c : P, slots],
                        start=(c == 0),
                        stop=(c == PASSES - 1),
                    )
                y, origin = results[e]
                nc.scalar.activation(
                    y[:, e * C - origin : (e + 1) * C - origin], acc[:], RELU, bias=bias[:, e : e + 1]
                )
                experts = e + 1
                z = experts * C
                if z % SCATTER == 0:
                    a = z - SCATTER
                    nc.vector.tensor_tensor(
                        scattered[:].indirect(offsets[:, a // LIST : z // LIST]),
                        y[:, a - origin : z - origin],
                        gate_all[:, a:z],
                        MULT,
                    )

        summed = keep.tile([P, T], F32, name="summed")
        for lo, hi in ADDS:
            nc.vector.tensor_tensor(summed[:, lo:hi], scattered[:, lo:hi], residual[:, lo:hi], ADD)
            nc.sync.dma_start(out=out[:, lo:hi], in_=summed[:, lo:hi])
